import numpy as np
import ml_dtypes


def mxq(x, axis, fmt="e4m3"):
    dtype, down = {"e4m3": (ml_dtypes.float8_e4m3fn, 7), "e5m2": (ml_dtypes.float8_e5m2, 14)}[fmt]
    v = np.moveaxis(np.asarray(x, np.float32).astype(ml_dtypes.bfloat16).astype(np.float64), axis, -1)
    blocks = v.reshape(v.shape[:-1] + (-1, 32))
    amax = np.abs(blocks).max(-1, keepdims=True)
    byte = np.maximum(np.where(amax > 0, np.frexp(amax)[1] - 1 + 127, 0) - down, 1)
    scale = np.exp2(byte - 127.0)
    codes = (blocks / scale).astype(np.float32).astype(dtype).astype(np.float64)
    return np.moveaxis((codes * scale).reshape(v.shape), -1, axis)


WIDE = False


def mx_kscale(k):
    if not WIDE:
        return np.ones(k)
    levels = np.array([10, -10, 5, -5, 0])
    if k % 512:
        return np.exp2(np.random.permutation(np.resize(levels, k // 32))).repeat(32)
    a = np.empty((k // 512, 16))
    for p in range(k // 512):
        a[p, :8] = np.random.permutation(np.resize(levels, 8))
        for g in range(8):
            far = levels[np.abs(levels - a[p, g]) >= 10]
            a[p, g + 8] = far[np.random.randint(len(far))]
    return np.exp2(a.ravel()).repeat(32)


def f64(x):
    return np.asarray(x).astype(np.float64)


def striped(idx):
    return np.tile(idx.reshape(-1, 16).T, (8, 1)).astype(np.uint16)


def unstriped(offs):
    return offs[:16].T.reshape(-1).astype(np.int64)


def pack_weight(w):
    k, n = w.shape
    w = f64(np.asarray(w, np.float32).astype(ml_dtypes.bfloat16)).reshape(k // 32, 32, n)
    amax = np.abs(w).max(1)
    byte = np.clip(np.where(amax > 0, np.frexp(amax)[1] - 1 + 127 - 7, 1), 1, 254)
    scaled = (w * np.exp2(127.0 - byte)[:, None, :]).reshape(k, n).astype(np.float32)
    words = np.ascontiguousarray(scaled.reshape(k // 512, 128, 4, n).transpose(0, 1, 3, 2)).astype(ml_dtypes.float8_e4m3fn).view(np.uint8)
    return words, np.ascontiguousarray(byte.astype(np.uint8).reshape(k // 512, 16, n))


def unpack_weight(words, scales):
    g, p, n, _ = words.shape
    vals = np.ascontiguousarray(words).view(ml_dtypes.float8_e4m3fn).astype(np.float64) * np.repeat(np.exp2(scales.astype(np.float64) - 127.0), 8, axis=1)[..., None]
    return vals.transpose(0, 1, 3, 2).reshape(g * 512, n)


K, T, S, D, N, V = 512, 2048, 1024, 2, 128, 512


def setup_inputs():
    n = np.random.standard_normal
    s = mx_kscale(K)[:, None]
    packed_xT = pack_weight(n((K, T)) * s)
    return {
        "x_words": packed_xT[0],
        "x_scales": packed_xT[1],
        "w1": (n((K, N)) / np.sqrt(K) / s).astype(np.float32),
        "w2": (n((K, N)) / np.sqrt(K) / s).astype(np.float32),
        "w3": (n((K, N)) / np.sqrt(K) / s).astype(np.float32),
        "w4": (n((K, N)) / np.sqrt(K) / s).astype(np.float32),
        "offs": striped(np.random.permutation(T)[:S]),
        "parent": striped(np.random.permutation(T)[:V]),
    }


def reference(x_words, x_scales, w1, w2, w3, w4, offs, parent):
    x_parent = unpack_weight(x_words, x_scales)[:, unstriped(parent)]
    h = mxq(f64(w3), 0, "e4m3").T @ x_parent
    wv = np.exp(mxq(f64(w4), 0, "e4m3").T @ x_parent)
    xq = unpack_weight(x_words, x_scales)[:, unstriped(offs)]
    y = mxq(f64(w1), 0, "e4m3").T @ xq
    va = np.exp(mxq(f64(w2), 0, "e4m3").T @ xq)
    gg = (h - (y.reshape(len(y), -1, D).sum(axis=2))) / (wv + va.reshape(len(va), -1, D).sum(axis=2))
    return h - (wv * gg)

@@ -1,0 +1,164 @@
+from contextlib import ExitStack
+
+import concourse.mybir as mybir
+
+K, T, S, V, M = 512, 2048, 1024, 512, 128
+FLOPS = 2 * K * M * (2 * S + 2 * V)
+
+F32 = mybir.dt.float32
+BF16 = mybir.dt.bfloat16
+I32 = mybir.dt.int32
+U32 = mybir.dt.uint32
+U16 = mybir.dt.uint16
+U8 = mybir.dt.uint8
+FP8X4 = mybir.dt.float8_e4m3fn_x4
+ACT = mybir.ActivationFunctionType
+ADD = mybir.AluOpType.add
+MULT = mybir.AluOpType.mult
+
+P = 128
+PACK = 4
+LEAF_PIECES = ((0, 512), (512, 768), (768, 1024))
+HALF = V // 2
+
+
+def tile_picked_yrecon_top_p_kernel(
+    tc, x_words, x_scales, w1, w2, w3, w4, offs, parent, out
+):
+    nc = tc.nc
+    with ExitStack() as ctx:
+        keep = ctx.enter_context(tc.tile_pool(name="keep", bufs=1))
+        psum = ctx.enter_context(tc.psum_pool(name="psum", bufs=1))
+
+        parent_list = keep.tile([P, V // 16], U16, name="parent_list")
+        leaf_list = keep.tile([P, S // 16], U16, name="leaf_list")
+        store_scales = keep.tile([P, T], U8, name="store_scales", align_bytes=64)
+        store_words = keep.tile([P, T], U32, name="store_words", align_bytes=64)
+
+        nc.vector.memset(store_scales[:].bitcast(I32), 0)
+        nc.sync.dma_start(parent_list[:], parent)
+        nc.sync.dma_start(leaf_list[:], offs)
+        for q in range(4):
+            (nc.sync if q % 2 == 0 else nc.scalar).dma_start(
+                store_scales[32 * q : 32 * q + 4, :].bitcast(I32),
+                x_scales[0, 4 * q : 4 * q + 4, :].bitcast(I32),
+            )
+
+        raw = {}
+
+        def load_weight(name, w):
+            raw[name] = keep.tile([P, PACK, M], F32, name="raw_" + name)
+            nc.sync.dma_start(raw[name][:], w.rearrange("(p j) m -> p j m", j=PACK))
+
+        load_weight("w4", w4)
+        load_weight("w2", w2)
+        nc.sync.dma_start(
+            store_words[:].bitcast(I32),
+            x_words[0].rearrange("p n t -> p (n t)").bitcast(I32),
+        )
+        load_weight("w1", w1)
+        load_weight("w3", w3)
+
+        grouped, codes, scales = {}, {}, {}
+
+        def cast(name):
+            grouped[name] = keep.tile([P, M, PACK], BF16, name="grouped_" + name, tag="grouped_" + name, align_bytes=64)
+            nc.scalar.copy(
+                grouped[name][:].rearrange("p (c i) t -> p c t i", i=4),
+                raw[name][:].rearrange("p t (c i) -> p c t i", i=4),
+            )
+
+        def quantize(name):
+            codes[name] = keep.tile([P, M], U32, name="codes_" + name, align_bytes=64)
+            scales[name] = keep.tile([P, M], U8, name="scales_" + name, align_bytes=64)
+            nc.vector.quantize_mx(
+                out=codes[name][:].bitcast(FP8X4),
+                scales=scales[name][:],
+                in_=grouped[name][:].rearrange("p m t -> p (m t)"),
+            )
+
+        def product(acc, name, words, plane):
+            nc.tensor.matmul_mx(
+                out=acc,
+                lhsT=codes[name][:].bitcast(FP8X4),
+                lhsT_scale=scales[name][:],
+                rhs=words.bitcast(FP8X4),
+                rhs_scale=plane,
+                start=True,
+                stop=True,
+            )
+
+        for name in ("w4", "w2", "w1", "w3"):
+            cast(name)
+
+        parent_scales = keep.tile([P, V], U8, name="parent_scales", align_bytes=64)
+        leaf_scales = keep.tile([P, S], U8, name="leaf_scales", align_bytes=64)
+        nc.vector.tensor_copy(parent_scales[:], store_scales[:].indirect(parent_list[:]))
+        nc.vector.tensor_copy(leaf_scales[:], store_scales[:].indirect(leaf_list[:]))
+        for name in ("w4", "w2", "w1"):
+            quantize(name)
+
+        parent_words = keep.tile([P, V], U32, name="parent_words", align_bytes=64)
+        nc.vector.tensor_copy(parent_words[:], store_words[:].indirect(parent_list[:]))
+        leaf_words = []
+        for n, (a, b) in enumerate(LEAF_PIECES):
+            piece = keep.tile([P, b - a], U32, name="leaf_words%d" % n, tag="grouped_w1" if n == 1 else "leaf_words%d" % n, align_bytes=64)
+            nc.vector.tensor_copy(piece[:], store_words[:].indirect(leaf_list[:, a // 16 : b // 16]))
+            leaf_words.append(piece)
+
+        wv = keep.tile([P, V], F32, name="wv")
+        va = keep.tile([P, 2, V], F32, name="va")
+        y_odd = keep.tile([P, HALF], F32, name="y_odd")
+        log_wv = psum.tile([P, V], F32, name="log_wv")
+        product(log_wv[:], "w4", parent_words[:], parent_scales[:])
+        nc.scalar.activation(wv[:], log_wv[:], ACT.Exp)
+
+        y = [psum.tile([P, V], F32, name="y%d" % n) for n in range(2)]
+        for n, (a, b) in enumerate(LEAF_PIECES):
+            log_va = psum.tile([P, b - a], F32, name="log_va%d" % n)
+            product(log_va[:], "w2", leaf_words[n][:], leaf_scales[:, a:b])
+            product(y[a // V][:, a % V : a % V + b - a], "w1", leaf_words[n][:], leaf_scales[:, a:b])
+            nc.scalar.activation(
+                va[:, :, a // 2 : b // 2], log_va[:].rearrange("p (v d) -> p d v", d=2), ACT.Exp
+            )
+            if n == 0:
+                nc.scalar.copy(y_odd[:], y[0][:, 1::2])
+
+        warm = keep.tile([P, 1], F32, name="warm")
+        nc.scalar.activation(warm[:], va[:, 1, V - 1 : V], ACT.Abs_reciprocal_sqrt)
+
+        quantize("w3")
+        h = psum.tile([P, V], F32, name="h")
+        product(h[:], "w3", parent_words[:], parent_scales[:])
+
+        va_sum = keep.tile([P, V], F32, name="va_sum")
+        y_sum = keep.tile([P, V], F32, name="y_sum")
+        total = keep.tile([P, V], F32, name="total")
+        h_part = keep.tile([P, V], F32, name="h_part")
+        y_part = keep.tile([P, V], F32, name="y_part")
+        numerator = keep.tile([P, V], F32, name="numerator")
+        inv_root = keep.tile([P, V], F32, name="inv_root")
+        inv_total = keep.tile([P, V], F32, name="inv_total")
+        result = keep.tile([P, V], F32, name="result")
+
+        early, late = slice(0, 384), slice(384, V)
+        lo, hi = slice(0, HALF), slice(HALF, V)
+        nc.vector.tensor_tensor(y_sum[:, lo], y[0][:, 0::2], y_odd[:], ADD)
+        nc.vector.tensor_tensor(va_sum[:, early], va[:, 0, early], va[:, 1, early], ADD)
+        nc.vector.tensor_tensor(y_part[:, lo], y_sum[:, lo], wv[:, lo], MULT)
+        nc.vector.tensor_tensor(va_sum[:, late], va[:, 0, late], va[:, 1, late], ADD)
+        nc.vector.tensor_reduce(
+            out=y_sum[:, hi], in_=y[1][:].rearrange("p (v d) -> p v d", d=2), op=ADD, axis=mybir.AxisListType.X
+        )
+        nc.vector.tensor_tensor(total[:], va_sum[:], wv[:], ADD)
+        nc.vector.tensor_tensor(h_part[:], h[:], va_sum[:], MULT)
+        nc.vector.tensor_tensor(y_part[:, hi], y_sum[:, hi], wv[:, hi], MULT)
+        for cols in (lo, hi):
+            nc.vector.tensor_tensor(numerator[:, cols], h_part[:, cols], y_part[:, cols], ADD)
+        for cols in (lo, hi):
+            nc.scalar.activation(inv_root[:, cols], total[:, cols], ACT.Abs_reciprocal_sqrt)
+        for cols in (lo, hi):
+            nc.scalar.activation(inv_total[:, cols], inv_root[:, cols], ACT.Square)
+        for cols in (lo, hi):
+            nc.vector.tensor_tensor(result[:, cols], numerator[:, cols], inv_total[:, cols], MULT)
+            nc.sync.dma_start(out[:, cols], result[:, cols])

@@ -15,10 +15,14 @@ FP8X4 = mybir.dt.float8_e4m3fn_x4
 ACT = mybir.ActivationFunctionType
 ADD = mybir.AluOpType.add
 MULT = mybir.AluOpType.mult
+MIN = mybir.AluOpType.min
+MAX = mybir.AluOpType.max
 
 P = 128
 PACK = 4
-LEAF_PIECES = ((0, 512), (512, 768), (768, 1024))
+D = 2
+PIECES = ((0, 256), (256, 384), (384, 512))
+RATIO_BOUND = 2.0**60
 HALF = V // 2
 
 
@@ -36,40 +40,47 @@ def tile_picked_yrecon_top_p_kernel(
         store_words = keep.tile([P, T], U32, name="store_words", align_bytes=64)
 
         nc.vector.memset(store_scales[:].bitcast(I32), 0)
-        nc.sync.dma_start(parent_list[:], parent)
         nc.sync.dma_start(leaf_list[:], offs)
+        nc.sync.dma_start(parent_list[:], parent)
+        nc.sync.dma_start(store_scales[0:P:8, :].bitcast(I32), x_scales[0].bitcast(I32))
+        placed_scales = keep.tile([P, T], U8, name="placed_scales", align_bytes=64)
+        nc.vector.memset(placed_scales[:].bitcast(I32), 0)
         for q in range(4):
-            (nc.sync if q % 2 == 0 else nc.scalar).dma_start(
-                store_scales[32 * q : 32 * q + 4, :].bitcast(I32),
+            nc.sync.dma_start(
+                placed_scales[32 * q : 32 * q + 4, :].bitcast(I32),
                 x_scales[0, 4 * q : 4 * q + 4, :].bitcast(I32),
             )
+        leaf_scales = keep.tile([P, S], U8, name="leaf_scales", align_bytes=64)
+        nc.vector.memset(leaf_scales[:].bitcast(I32), 0)
 
         raw = {}
 
         def load_weight(name, w):
-            raw[name] = keep.tile([P, PACK, M], F32, name="raw_" + name)
+            raw[name] = keep.tile([P, PACK, M], F32, name="raw_" + name, tag="raw_" + name)
             nc.sync.dma_start(raw[name][:], w.rearrange("(p j) m -> p j m", j=PACK))
 
         load_weight("w4", w4)
-        load_weight("w2", w2)
         nc.sync.dma_start(
             store_words[:].bitcast(I32),
             x_words[0].rearrange("p n t -> p (n t)").bitcast(I32),
         )
-        load_weight("w1", w1)
+        load_weight("w2", w2)
         load_weight("w3", w3)
+        load_weight("w1", w1)
 
         grouped, codes, scales = {}, {}, {}
 
         def cast(name):
             grouped[name] = keep.tile([P, M, PACK], BF16, name="grouped_" + name, tag="grouped_" + name, align_bytes=64)
-            nc.scalar.copy(
+            nc.scalar.activation(
                 grouped[name][:].rearrange("p (c i) t -> p c t i", i=4),
                 raw[name][:].rearrange("p t (c i) -> p c t i", i=4),
+                ACT.Copy,
+                scale=-1.0 if name == "w4" else 1.0,
             )
 
-        def quantize(name):
-            codes[name] = keep.tile([P, M], U32, name="codes_" + name, align_bytes=64)
+        def quantize(name, slot):
+            codes[name] = keep.tile([P, M], U32, name="codes_" + name, tag=slot, align_bytes=64)
             scales[name] = keep.tile([P, M], U8, name="scales_" + name, align_bytes=64)
             nc.vector.quantize_mx(
                 out=codes[name][:].bitcast(FP8X4),
@@ -77,88 +88,113 @@ def tile_picked_yrecon_top_p_kernel(
                 in_=grouped[name][:].rearrange("p m t -> p (m t)"),
             )
 
-        def product(acc, name, words, plane):
+        def product(acc, name, words, plane, start, stop):
             nc.tensor.matmul_mx(
                 out=acc,
                 lhsT=codes[name][:].bitcast(FP8X4),
                 lhsT_scale=scales[name][:],
                 rhs=words.bitcast(FP8X4),
                 rhs_scale=plane,
-                start=True,
-                stop=True,
+                start=start,
+                stop=stop,
             )
 
-        for name in ("w4", "w2", "w1", "w3"):
+        for name in ("w4", "w2", "w3", "w1"):
             cast(name)
 
+        picked_rows = keep.tile([P, S], U8, name="picked_rows", align_bytes=64)
+        sorted_rows = keep.tile([P, S], U8, name="sorted_rows", align_bytes=64)
         parent_scales = keep.tile([P, V], U8, name="parent_scales", align_bytes=64)
-        leaf_scales = keep.tile([P, S], U8, name="leaf_scales", align_bytes=64)
-        nc.vector.tensor_copy(parent_scales[:], store_scales[:].indirect(parent_list[:]))
-        nc.vector.tensor_copy(leaf_scales[:], store_scales[:].indirect(leaf_list[:]))
-        for name in ("w4", "w2", "w1"):
-            quantize(name)
-
         parent_words = keep.tile([P, V], U32, name="parent_words", align_bytes=64)
+        nc.vector.tensor_copy(picked_rows[:], store_scales[:].indirect(leaf_list[:]))
+        nc.vector.tensor_copy(
+            sorted_rows[:].rearrange("p (d v) -> p d v", d=D), picked_rows[:].rearrange("p (v d) -> p d v", d=D)
+        )
+        for i in range(4):
+            nc.sync.dma_start(leaf_scales[i:P:32, :].bitcast(I32), sorted_rows[8 * i : P : 32, :].bitcast(I32))
+        nc.vector.tensor_copy(parent_scales[:], placed_scales[:].indirect(parent_list[:]))
+        quantize("w4", "codes_w4")
         nc.vector.tensor_copy(parent_words[:], store_words[:].indirect(parent_list[:]))
-        leaf_words = []
-        for n, (a, b) in enumerate(LEAF_PIECES):
-            piece = keep.tile([P, b - a], U32, name="leaf_words%d" % n, tag="grouped_w1" if n == 1 else "leaf_words%d" % n, align_bytes=64)
-            nc.vector.tensor_copy(piece[:], store_words[:].indirect(leaf_list[:, a // 16 : b // 16]))
-            leaf_words.append(piece)
 
-        wv = keep.tile([P, V], F32, name="wv")
-        va = keep.tile([P, 2, V], F32, name="va")
-        y_odd = keep.tile([P, HALF], F32, name="y_odd")
-        log_wv = psum.tile([P, V], F32, name="log_wv")
-        product(log_wv[:], "w4", parent_words[:], parent_scales[:])
-        nc.scalar.activation(wv[:], log_wv[:], ACT.Exp)
+        lo, hi = slice(0, HALF), slice(HALF, V)
 
-        y = [psum.tile([P, V], F32, name="y%d" % n) for n in range(2)]
-        for n, (a, b) in enumerate(LEAF_PIECES):
-            log_va = psum.tile([P, b - a], F32, name="log_va%d" % n)
-            product(log_va[:], "w2", leaf_words[n][:], leaf_scales[:, a:b])
-            product(y[a // V][:, a % V : a % V + b - a], "w1", leaf_words[n][:], leaf_scales[:, a:b])
-            nc.scalar.activation(
-                va[:, :, a // 2 : b // 2], log_va[:].rearrange("p (v d) -> p d v", d=2), ACT.Exp
+        def gather_leaves(words, first, a, b):
+            nc.vector.tensor_copy(
+                words[:, :, a - first : b - first].rearrange("p d v -> p v d"),
+                store_words[:].indirect(leaf_list[:, D * a // 16 : D * b // 16]),
             )
-            if n == 0:
-                nc.scalar.copy(y_odd[:], y[0][:, 1::2])
 
-        warm = keep.tile([P, 1], F32, name="warm")
-        nc.scalar.activation(warm[:], va[:, 1, V - 1 : V], ACT.Abs_reciprocal_sqrt)
+        lo_words = keep.tile([P, D, HALF], U32, name="lo_words", align_bytes=64)
+        gather_leaves(lo_words, 0, *PIECES[0])
+        quantize("w2", "codes_w2")
+        hi_words = keep.tile([P, D, HALF], U32, name="hi_words", tag="grouped_w2", align_bytes=64)
+        gather_leaves(hi_words, HALF, *PIECES[1])
+        gather_leaves(hi_words, HALF, *PIECES[2])
 
-        quantize("w3")
-        h = psum.tile([P, V], F32, name="h")
-        product(h[:], "w3", parent_words[:], parent_scales[:])
+        def leaf_operand(d, a, b):
+            words, first = (lo_words, 0) if a < HALF else (hi_words, HALF)
+            return words[:, d, a - first : b - first], leaf_scales[:, d * V + a : d * V + b]
 
-        va_sum = keep.tile([P, V], F32, name="va_sum")
-        y_sum = keep.tile([P, V], F32, name="y_sum")
-        total = keep.tile([P, V], F32, name="total")
+        log_ratio = {}
+        for n, (a, b) in enumerate(PIECES):
+            for d in range(D):
+                bank = "log_ratio%d%d" % (n, d)
+                log_ratio[n, d] = psum.tile([P, b - a], F32, name=bank, tag=bank)
+                product(log_ratio[n, d][:], "w4", parent_words[:, a:b], parent_scales[:, a:b], True, False)
+
+        ratio_lo = [
+            keep.tile([P, HALF], F32, name="ratio_lo%d" % d, tag="ratio_lo%d" % d, align_bytes=64) for d in range(D)
+        ]
+        ratio_hi = [keep.tile([P, HALF], F32, name="ratio_hi%d" % d, tag="ratio_hi%d" % d) for d in range(D)]
+        for n, (a, b) in enumerate(PIECES):
+            for d in range(D):
+                product(log_ratio[n, d][:], "w2", *leaf_operand(d, a, b), False, True)
+                ratio = ratio_lo[d][:] if n == 0 else ratio_hi[d][:, a - HALF : b - HALF]
+                nc.scalar.activation(ratio, log_ratio[n, d][:], ACT.Exp)
+
+        ratio_sum = keep.tile([P, V], F32, name="ratio_sum")
+        squared = keep.tile([P, V], F32, name="squared")
         h_part = keep.tile([P, V], F32, name="h_part")
-        y_part = keep.tile([P, V], F32, name="y_part")
-        numerator = keep.tile([P, V], F32, name="numerator")
-        inv_root = keep.tile([P, V], F32, name="inv_root")
         inv_total = keep.tile([P, V], F32, name="inv_total")
         result = keep.tile([P, V], F32, name="result")
 
-        early, late = slice(0, 384), slice(384, V)
-        lo, hi = slice(0, HALF), slice(HALF, V)
-        nc.vector.tensor_tensor(y_sum[:, lo], y[0][:, 0::2], y_odd[:], ADD)
-        nc.vector.tensor_tensor(va_sum[:, early], va[:, 0, early], va[:, 1, early], ADD)
-        nc.vector.tensor_tensor(y_part[:, lo], y_sum[:, lo], wv[:, lo], MULT)
-        nc.vector.tensor_tensor(va_sum[:, late], va[:, 0, late], va[:, 1, late], ADD)
-        nc.vector.tensor_reduce(
-            out=y_sum[:, hi], in_=y[1][:].rearrange("p (v d) -> p v d", d=2), op=ADD, axis=mybir.AxisListType.X
-        )
-        nc.vector.tensor_tensor(total[:], va_sum[:], wv[:], ADD)
-        nc.vector.tensor_tensor(h_part[:], h[:], va_sum[:], MULT)
-        nc.vector.tensor_tensor(y_part[:, hi], y_sum[:, hi], wv[:, hi], MULT)
-        for cols in (lo, hi):
-            nc.vector.tensor_tensor(numerator[:, cols], h_part[:, cols], y_part[:, cols], ADD)
-        for cols in (lo, hi):
-            nc.scalar.activation(inv_root[:, cols], total[:, cols], ACT.Abs_reciprocal_sqrt)
-        for cols in (lo, hi):
-            nc.scalar.activation(inv_total[:, cols], inv_root[:, cols], ACT.Square)
-        for cols in (lo, hi):
-            nc.vector.tensor_tensor(result[:, cols], numerator[:, cols], inv_total[:, cols], MULT)
-            nc.sync.dma_start(out[:, cols], result[:, cols])
+        def add_ratios(cols, ratio):
+            nc.vector.tensor_tensor(ratio_sum[:, cols], ratio[0][:], ratio[1][:], ADD)
+
+        def square(cols):
+            nc.vector.scalar_tensor_tensor(squared[:, cols], ratio_sum[:, cols], 2.0, ratio_sum[:, cols], ADD, MULT)
+
+        def weigh_h(cols):
+            nc.vector.scalar_tensor_tensor(h_part[:, cols], ratio_sum[:, cols], RATIO_BOUND, h[:, cols], MIN, MULT)
+
+        add_ratios(lo, ratio_lo)
+        quantize("w3", "ratio_lo0")
+        square(lo)
+        quantize("w1", "ratio_lo1")
+
+        h = psum.tile([P, V], F32, name="h")
+        product(h[:], "w3", parent_words[:], parent_scales[:], True, True)
+        y_sum = [psum.tile([P, HALF], F32, name="y_sum%d" % n, tag="log_ratio0%d" % n) for n in range(2)]
+        for n, cols in enumerate((lo, hi)):
+            for d in range(D):
+                product(y_sum[n][:], "w1", *leaf_operand(d, cols.start, cols.stop), d == 0, d == D - 1)
+
+        add_ratios(hi, ratio_hi)
+        weigh_h(lo)
+        square(hi)
+        numerator = [keep.tile([P, HALF], F32, name="numerator%d" % n, tag="ratio_hi%d" % n) for n in range(2)]
+        weigh_h(hi)
+        for n, cols in enumerate((lo, hi)):
+            nc.vector.tensor_tensor(numerator[n][:], y_sum[n][:], h_part[:, cols], ADD)
+        for a, b in PIECES:
+            nc.scalar.activation(inv_total[:, a:b], squared[:, a:b], ACT.Abs_reciprocal_sqrt, bias=1.0)
+        for a, b in PIECES:
+            nc.vector.scalar_tensor_tensor(
+                result[:, a:b],
+                inv_total[:, a:b],
+                1.0 / RATIO_BOUND,
+                numerator[a // HALF][:, a % HALF : a % HALF + b - a],
+                MAX,
+                MULT,
+            )
+            nc.sync.dma_start(out[:, a:b], result[:, a:b])

@@ -3,6 +3,7 @@ from contextlib import ExitStack
 import concourse.mybir as mybir
 
 K, T, S, V, M = 512, 2048, 1024, 512, 128
+D = 2
 FLOPS = 2 * K * M * (2 * S + 2 * V)
 
 F32 = mybir.dt.float32
@@ -20,10 +21,16 @@ MAX = mybir.AluOpType.max
 
 P = 128
 PACK = 4
-D = 2
-PIECES = ((0, 256), (256, 384), (384, 512))
-RATIO_BOUND = 2.0**60
+QUADRANT = 32
+ROWS = 4
+BLOCK = 8
+COLUMN = 16
+RUN = 4
 HALF = V // 2
+
+PIECES = ((0, HALF), (HALF, HALF + V // 4), (HALF + V // 4, V))
+
+RATIO_BOUND = 2.0**60
 
 
 def tile_picked_yrecon_top_p_kernel(
@@ -34,21 +41,21 @@ def tile_picked_yrecon_top_p_kernel(
         keep = ctx.enter_context(tc.tile_pool(name="keep", bufs=1))
         psum = ctx.enter_context(tc.psum_pool(name="psum", bufs=1))
 
-        parent_list = keep.tile([P, V // 16], U16, name="parent_list")
-        leaf_list = keep.tile([P, S // 16], U16, name="leaf_list")
-        store_scales = keep.tile([P, T], U8, name="store_scales", align_bytes=64)
+        parent_list = keep.tile([P, V // COLUMN], U16, name="parent_list")
+        leaf_list = keep.tile([P, S // COLUMN], U16, name="leaf_list")
+        spread_scales = keep.tile([P, T], U8, name="spread_scales", align_bytes=64)
         store_words = keep.tile([P, T], U32, name="store_words", align_bytes=64)
 
-        nc.vector.memset(store_scales[:].bitcast(I32), 0)
+        nc.vector.memset(spread_scales[:].bitcast(I32), 0)
         nc.sync.dma_start(leaf_list[:], offs)
         nc.sync.dma_start(parent_list[:], parent)
-        nc.sync.dma_start(store_scales[0:P:8, :].bitcast(I32), x_scales[0].bitcast(I32))
+        nc.sync.dma_start(spread_scales[0:P:BLOCK, :].bitcast(I32), x_scales[0].bitcast(I32))
         placed_scales = keep.tile([P, T], U8, name="placed_scales", align_bytes=64)
         nc.vector.memset(placed_scales[:].bitcast(I32), 0)
-        for q in range(4):
+        for q in range(P // QUADRANT):
             nc.sync.dma_start(
-                placed_scales[32 * q : 32 * q + 4, :].bitcast(I32),
-                x_scales[0, 4 * q : 4 * q + 4, :].bitcast(I32),
+                placed_scales[QUADRANT * q : QUADRANT * q + ROWS, :].bitcast(I32),
+                x_scales[0, ROWS * q : ROWS * (q + 1), :].bitcast(I32),
             )
         leaf_scales = keep.tile([P, S], U8, name="leaf_scales", align_bytes=64)
         nc.vector.memset(leaf_scales[:].bitcast(I32), 0)
@@ -56,84 +63,95 @@ def tile_picked_yrecon_top_p_kernel(
         raw = {}
 
         def load_weight(name, w):
-            raw[name] = keep.tile([P, PACK, M], F32, name="raw_" + name, tag="raw_" + name)
-            nc.sync.dma_start(raw[name][:], w.rearrange("(p j) m -> p j m", j=PACK))
+            raw[name] = keep.tile([P, PACK, M], F32, name="raw_" + name)
+            nc.sync.dma_start(raw[name][:], w.rearrange("(p t) m -> p t m", t=PACK))
 
         load_weight("w4", w4)
+        load_weight("w2", w2)
         nc.sync.dma_start(
             store_words[:].bitcast(I32),
             x_words[0].rearrange("p n t -> p (n t)").bitcast(I32),
         )
-        load_weight("w2", w2)
         load_weight("w3", w3)
         load_weight("w1", w1)
 
-        grouped, codes, scales = {}, {}, {}
+        codes, scales = {}, {}
 
-        def cast(name):
-            grouped[name] = keep.tile([P, M, PACK], BF16, name="grouped_" + name, tag="grouped_" + name, align_bytes=64)
-            nc.scalar.activation(
-                grouped[name][:].rearrange("p (c i) t -> p c t i", i=4),
-                raw[name][:].rearrange("p t (c i) -> p c t i", i=4),
-                ACT.Copy,
-                scale=-1.0 if name == "w4" else 1.0,
-            )
+        def cast_pair(names):
+            grouped = keep.tile([P, len(names), M, PACK], BF16, name="grouped_" + names[0], align_bytes=64)
+            for n, name in enumerate(names):
+                nc.scalar.activation(
+                    grouped[:, n].rearrange("p (c i) t -> p c t i", i=RUN),
+                    raw[name][:].rearrange("p t (c i) -> p c t i", i=RUN),
+                    ACT.Copy,
+                    scale=-1.0 if name == "w4" else 1.0,
+                )
+            return grouped
 
-        def quantize(name, slot):
-            codes[name] = keep.tile([P, M], U32, name="codes_" + name, tag=slot, align_bytes=64)
-            scales[name] = keep.tile([P, M], U8, name="scales_" + name, align_bytes=64)
+        def quantize_pair(names, grouped):
+            pair_codes = keep.tile([P, len(names) * M], U32, name="codes_" + names[0], align_bytes=64)
+            pair_scales = keep.tile([P, len(names) * M], U8, name="scales_" + names[0], align_bytes=64)
             nc.vector.quantize_mx(
-                out=codes[name][:].bitcast(FP8X4),
-                scales=scales[name][:],
-                in_=grouped[name][:].rearrange("p m t -> p (m t)"),
+                out=pair_codes[:].bitcast(FP8X4),
+                scales=pair_scales[:],
+                in_=grouped[:].rearrange("p n m t -> p (n m t)"),
             )
+            for n, name in enumerate(names):
+                codes[name] = pair_codes[:, n * M : (n + 1) * M]
+                scales[name] = pair_scales[:, n * M : (n + 1) * M]
 
-        def product(acc, name, words, plane, start, stop):
+        def product(acc, name, column_words, column_scales, start, stop):
             nc.tensor.matmul_mx(
                 out=acc,
-                lhsT=codes[name][:].bitcast(FP8X4),
-                lhsT_scale=scales[name][:],
-                rhs=words.bitcast(FP8X4),
-                rhs_scale=plane,
+                lhsT=codes[name].bitcast(FP8X4),
+                lhsT_scale=scales[name],
+                rhs=column_words.bitcast(FP8X4),
+                rhs_scale=column_scales,
                 start=start,
                 stop=stop,
             )
 
-        for name in ("w4", "w2", "w3", "w1"):
-            cast(name)
+        def leaves_of(a, b):
+            return leaf_list[:, D * a // COLUMN : D * b // COLUMN]
+
+        variance_weights = cast_pair(("w4", "w2"))
+        forecast_weights = cast_pair(("w3", "w1"))
 
         picked_rows = keep.tile([P, S], U8, name="picked_rows", align_bytes=64)
         sorted_rows = keep.tile([P, S], U8, name="sorted_rows", align_bytes=64)
         parent_scales = keep.tile([P, V], U8, name="parent_scales", align_bytes=64)
         parent_words = keep.tile([P, V], U32, name="parent_words", align_bytes=64)
-        nc.vector.tensor_copy(picked_rows[:], store_scales[:].indirect(leaf_list[:]))
-        nc.vector.tensor_copy(
-            sorted_rows[:].rearrange("p (d v) -> p d v", d=D), picked_rows[:].rearrange("p (v d) -> p d v", d=D)
-        )
-        for i in range(4):
-            nc.sync.dma_start(leaf_scales[i:P:32, :].bitcast(I32), sorted_rows[8 * i : P : 32, :].bitcast(I32))
+        for a in (0, HALF):
+            nc.vector.tensor_copy(
+                picked_rows[:, D * a : D * (a + HALF)], spread_scales[:].indirect(leaves_of(a, a + HALF))
+            )
+        for a in (0, HALF):
+            nc.vector.tensor_copy(
+                sorted_rows[:].rearrange("p (d v) -> p d v", d=D)[:, :, a : a + HALF],
+                picked_rows[:, D * a : D * (a + HALF)].rearrange("p (v d) -> p d v", d=D),
+            )
+        for i in range(ROWS):
+            nc.sync.dma_start(
+                leaf_scales[i:P:QUADRANT, :].bitcast(I32), sorted_rows[BLOCK * i : P : QUADRANT, :].bitcast(I32)
+            )
         nc.vector.tensor_copy(parent_scales[:], placed_scales[:].indirect(parent_list[:]))
-        quantize("w4", "codes_w4")
+        quantize_pair(("w4", "w2"), variance_weights)
+
         nc.vector.tensor_copy(parent_words[:], store_words[:].indirect(parent_list[:]))
 
         lo, hi = slice(0, HALF), slice(HALF, V)
+        leaf_words = [keep.tile([P, D, HALF], U32, name="leaf_words%d" % n, align_bytes=64) for n in range(2)]
 
-        def gather_leaves(words, first, a, b):
+        def words_under(a, b):
+            return leaf_words[a // HALF][:, :, a % HALF : a % HALF + b - a]
+
+        for a, b in PIECES:
             nc.vector.tensor_copy(
-                words[:, :, a - first : b - first].rearrange("p d v -> p v d"),
-                store_words[:].indirect(leaf_list[:, D * a // 16 : D * b // 16]),
+                words_under(a, b).rearrange("p d v -> p v d"), store_words[:].indirect(leaves_of(a, b))
             )
 
-        lo_words = keep.tile([P, D, HALF], U32, name="lo_words", align_bytes=64)
-        gather_leaves(lo_words, 0, *PIECES[0])
-        quantize("w2", "codes_w2")
-        hi_words = keep.tile([P, D, HALF], U32, name="hi_words", tag="grouped_w2", align_bytes=64)
-        gather_leaves(hi_words, HALF, *PIECES[1])
-        gather_leaves(hi_words, HALF, *PIECES[2])
-
         def leaf_operand(d, a, b):
-            words, first = (lo_words, 0) if a < HALF else (hi_words, HALF)
-            return words[:, d, a - first : b - first], leaf_scales[:, d * V + a : d * V + b]
+            return words_under(a, b)[:, d, :], leaf_scales[:, d * V + a : d * V + b]
 
         log_ratio = {}
         for n, (a, b) in enumerate(PIECES):
@@ -142,15 +160,13 @@ def tile_picked_yrecon_top_p_kernel(
                 log_ratio[n, d] = psum.tile([P, b - a], F32, name=bank, tag=bank)
                 product(log_ratio[n, d][:], "w4", parent_words[:, a:b], parent_scales[:, a:b], True, False)
 
-        ratio_lo = [
-            keep.tile([P, HALF], F32, name="ratio_lo%d" % d, tag="ratio_lo%d" % d, align_bytes=64) for d in range(D)
-        ]
+        ratio_lo = [keep.tile([P, HALF], F32, name="ratio_lo%d" % d) for d in range(D)]
         ratio_hi = [keep.tile([P, HALF], F32, name="ratio_hi%d" % d, tag="ratio_hi%d" % d) for d in range(D)]
         for n, (a, b) in enumerate(PIECES):
             for d in range(D):
                 product(log_ratio[n, d][:], "w2", *leaf_operand(d, a, b), False, True)
-                ratio = ratio_lo[d][:] if n == 0 else ratio_hi[d][:, a - HALF : b - HALF]
-                nc.scalar.activation(ratio, log_ratio[n, d][:], ACT.Exp)
+                ratio = (ratio_lo, ratio_hi)[a // HALF][d]
+                nc.scalar.activation(ratio[:, a % HALF : a % HALF + b - a], log_ratio[n, d][:], ACT.Exp)
 
         ratio_sum = keep.tile([P, V], F32, name="ratio_sum")
         squared = keep.tile([P, V], F32, name="squared")
@@ -158,8 +174,8 @@ def tile_picked_yrecon_top_p_kernel(
         inv_total = keep.tile([P, V], F32, name="inv_total")
         result = keep.tile([P, V], F32, name="result")
 
-        def add_ratios(cols, ratio):
-            nc.vector.tensor_tensor(ratio_sum[:, cols], ratio[0][:], ratio[1][:], ADD)
+        def add_ratios(cols, pair):
+            nc.vector.tensor_tensor(ratio_sum[:, cols], pair[0][:], pair[1][:], ADD)
 
         def square(cols):
             nc.vector.scalar_tensor_tensor(squared[:, cols], ratio_sum[:, cols], 2.0, ratio_sum[:, cols], ADD, MULT)
@@ -167,14 +183,16 @@ def tile_picked_yrecon_top_p_kernel(
         def weigh_h(cols):
             nc.vector.scalar_tensor_tensor(h_part[:, cols], ratio_sum[:, cols], RATIO_BOUND, h[:, cols], MIN, MULT)
 
+        quantize_pair(("w3", "w1"), forecast_weights)
         add_ratios(lo, ratio_lo)
-        quantize("w3", "ratio_lo0")
         square(lo)
-        quantize("w1", "ratio_lo1")
 
-        h = psum.tile([P, V], F32, name="h")
+        h = psum.tile([P, V], F32, name="h", tag="log_ratio00")
         product(h[:], "w3", parent_words[:], parent_scales[:], True, True)
-        y_sum = [psum.tile([P, HALF], F32, name="y_sum%d" % n, tag="log_ratio0%d" % n) for n in range(2)]
+        y_sum = [
+            psum.tile([P, HALF], F32, name="y_sum%d" % n, tag=bank)
+            for n, bank in enumerate(("log_ratio01", "log_ratio10"))
+        ]
         for n, cols in enumerate((lo, hi)):
             for d in range(D):
                 product(y_sum[n][:], "w1", *leaf_operand(d, cols.start, cols.stop), d == 0, d == D - 1)

from contextlib import ExitStack

import concourse.mybir as mybir

K, T, S, V, M = 512, 2048, 1024, 512, 128
D = 2
FLOPS = 2 * K * M * (2 * S + 2 * V)

F32 = mybir.dt.float32
BF16 = mybir.dt.bfloat16
I32 = mybir.dt.int32
U32 = mybir.dt.uint32
U16 = mybir.dt.uint16
U8 = mybir.dt.uint8
FP8X4 = mybir.dt.float8_e4m3fn_x4
ACT = mybir.ActivationFunctionType
ADD = mybir.AluOpType.add
MULT = mybir.AluOpType.mult
MIN = mybir.AluOpType.min
MAX = mybir.AluOpType.max

P = 128
PACK = 4
QUADRANT = 32
ROWS = 4
BLOCK = 8
COLUMN = 16
RUN = 4
HALF = V // 2

PIECES = ((0, HALF), (HALF, HALF + V // 4), (HALF + V // 4, V))

RATIO_BOUND = 2.0**60


def tile_picked_yrecon_top_p_kernel(
    tc, x_words, x_scales, w1, w2, w3, w4, offs, parent, out
):
    nc = tc.nc
    with ExitStack() as ctx:
        keep = ctx.enter_context(tc.tile_pool(name="keep", bufs=1))
        psum = ctx.enter_context(tc.psum_pool(name="psum", bufs=1))

        parent_list = keep.tile([P, V // COLUMN], U16, name="parent_list")
        leaf_list = keep.tile([P, S // COLUMN], U16, name="leaf_list")
        spread_scales = keep.tile([P, T], U8, name="spread_scales", align_bytes=64)
        store_words = keep.tile([P, T], U32, name="store_words", align_bytes=64)

        nc.vector.memset(spread_scales[:].bitcast(I32), 0)
        nc.sync.dma_start(leaf_list[:], offs)
        nc.sync.dma_start(parent_list[:], parent)
        nc.sync.dma_start(spread_scales[0:P:BLOCK, :].bitcast(I32), x_scales[0].bitcast(I32))
        placed_scales = keep.tile([P, T], U8, name="placed_scales", align_bytes=64)
        nc.vector.memset(placed_scales[:].bitcast(I32), 0)
        for q in range(P // QUADRANT):
            nc.sync.dma_start(
                placed_scales[QUADRANT * q : QUADRANT * q + ROWS, :].bitcast(I32),
                x_scales[0, ROWS * q : ROWS * (q + 1), :].bitcast(I32),
            )
        leaf_scales = keep.tile([P, S], U8, name="leaf_scales", align_bytes=64)
        nc.vector.memset(leaf_scales[:].bitcast(I32), 0)

        raw = {}

        def load_weight(name, w):
            raw[name] = keep.tile([P, PACK, M], F32, name="raw_" + name)
            nc.sync.dma_start(raw[name][:], w.rearrange("(p t) m -> p t m", t=PACK))

        load_weight("w4", w4)
        load_weight("w2", w2)
        nc.sync.dma_start(
            store_words[:].bitcast(I32),
            x_words[0].rearrange("p n t -> p (n t)").bitcast(I32),
        )
        load_weight("w3", w3)
        load_weight("w1", w1)

        codes, scales = {}, {}

        def cast_pair(names):
            grouped = keep.tile([P, len(names), M, PACK], BF16, name="grouped_" + names[0], align_bytes=64)
            for n, name in enumerate(names):
                nc.scalar.activation(
                    grouped[:, n].rearrange("p (c i) t -> p c t i", i=RUN),
                    raw[name][:].rearrange("p t (c i) -> p c t i", i=RUN),
                    ACT.Copy,
                    scale=-1.0 if name == "w4" else 1.0,
                )
            return grouped

        def quantize_pair(names, grouped):
            pair_codes = keep.tile([P, len(names) * M], U32, name="codes_" + names[0], align_bytes=64)
            pair_scales = keep.tile([P, len(names) * M], U8, name="scales_" + names[0], align_bytes=64)
            nc.vector.quantize_mx(
                out=pair_codes[:].bitcast(FP8X4),
                scales=pair_scales[:],
                in_=grouped[:].rearrange("p n m t -> p (n m t)"),
            )
            for n, name in enumerate(names):
                codes[name] = pair_codes[:, n * M : (n + 1) * M]
                scales[name] = pair_scales[:, n * M : (n + 1) * M]

        def product(acc, name, column_words, column_scales, start, stop):
            nc.tensor.matmul_mx(
                out=acc,
                lhsT=codes[name].bitcast(FP8X4),
                lhsT_scale=scales[name],
                rhs=column_words.bitcast(FP8X4),
                rhs_scale=column_scales,
                start=start,
                stop=stop,
            )

        def leaves_of(a, b):
            return leaf_list[:, D * a // COLUMN : D * b // COLUMN]

        variance_weights = cast_pair(("w4", "w2"))
        forecast_weights = cast_pair(("w3", "w1"))

        picked_rows = keep.tile([P, S], U8, name="picked_rows", align_bytes=64)
        sorted_rows = keep.tile([P, S], U8, name="sorted_rows", align_bytes=64)
        parent_scales = keep.tile([P, V], U8, name="parent_scales", align_bytes=64)
        parent_words = keep.tile([P, V], U32, name="parent_words", align_bytes=64)
        for a in (0, HALF):
            nc.vector.tensor_copy(
                picked_rows[:, D * a : D * (a + HALF)], spread_scales[:].indirect(leaves_of(a, a + HALF))
            )
        for a in (0, HALF):
            nc.vector.tensor_copy(
                sorted_rows[:].rearrange("p (d v) -> p d v", d=D)[:, :, a : a + HALF],
                picked_rows[:, D * a : D * (a + HALF)].rearrange("p (v d) -> p d v", d=D),
            )
        for i in range(ROWS):
            nc.sync.dma_start(
                leaf_scales[i:P:QUADRANT, :].bitcast(I32), sorted_rows[BLOCK * i : P : QUADRANT, :].bitcast(I32)
            )
        nc.vector.tensor_copy(parent_scales[:], placed_scales[:].indirect(parent_list[:]))
        quantize_pair(("w4", "w2"), variance_weights)

        nc.vector.tensor_copy(parent_words[:], store_words[:].indirect(parent_list[:]))

        lo, hi = slice(0, HALF), slice(HALF, V)
        leaf_words = [keep.tile([P, D, HALF], U32, name="leaf_words%d" % n, align_bytes=64) for n in range(2)]

        def words_under(a, b):
            return leaf_words[a // HALF][:, :, a % HALF : a % HALF + b - a]

        for a, b in PIECES:
            nc.vector.tensor_copy(
                words_under(a, b).rearrange("p d v -> p v d"), store_words[:].indirect(leaves_of(a, b))
            )

        def leaf_operand(d, a, b):
            return words_under(a, b)[:, d, :], leaf_scales[:, d * V + a : d * V + b]

        log_ratio = {}
        for n, (a, b) in enumerate(PIECES):
            for d in range(D):
                bank = "log_ratio%d%d" % (n, d)
                log_ratio[n, d] = psum.tile([P, b - a], F32, name=bank, tag=bank)
                product(log_ratio[n, d][:], "w4", parent_words[:, a:b], parent_scales[:, a:b], True, False)

        ratio_lo = [keep.tile([P, HALF], F32, name="ratio_lo%d" % d) for d in range(D)]
        ratio_hi = [keep.tile([P, HALF], F32, name="ratio_hi%d" % d, tag="ratio_hi%d" % d) for d in range(D)]
        for n, (a, b) in enumerate(PIECES):
            for d in range(D):
                product(log_ratio[n, d][:], "w2", *leaf_operand(d, a, b), False, True)
                ratio = (ratio_lo, ratio_hi)[a // HALF][d]
                nc.scalar.activation(ratio[:, a % HALF : a % HALF + b - a], log_ratio[n, d][:], ACT.Exp)

        ratio_sum = keep.tile([P, V], F32, name="ratio_sum")
        squared = keep.tile([P, V], F32, name="squared")
        h_part = keep.tile([P, V], F32, name="h_part")
        inv_total = keep.tile([P, V], F32, name="inv_total")
        result = keep.tile([P, V], F32, name="result")

        def add_ratios(cols, pair):
            nc.vector.tensor_tensor(ratio_sum[:, cols], pair[0][:], pair[1][:], ADD)

        def square(cols):
            nc.vector.scalar_tensor_tensor(squared[:, cols], ratio_sum[:, cols], 2.0, ratio_sum[:, cols], ADD, MULT)

        def weigh_h(cols):
            nc.vector.scalar_tensor_tensor(h_part[:, cols], ratio_sum[:, cols], RATIO_BOUND, h[:, cols], MIN, MULT)

        quantize_pair(("w3", "w1"), forecast_weights)
        add_ratios(lo, ratio_lo)
        square(lo)

        h = psum.tile([P, V], F32, name="h", tag="log_ratio00")
        product(h[:], "w3", parent_words[:], parent_scales[:], True, True)
        y_sum = [
            psum.tile([P, HALF], F32, name="y_sum%d" % n, tag=bank)
            for n, bank in enumerate(("log_ratio01", "log_ratio10"))
        ]
        for n, cols in enumerate((lo, hi)):
            for d in range(D):
                product(y_sum[n][:], "w1", *leaf_operand(d, cols.start, cols.stop), d == 0, d == D - 1)

        add_ratios(hi, ratio_hi)
        weigh_h(lo)
        square(hi)
        numerator = [keep.tile([P, HALF], F32, name="numerator%d" % n, tag="ratio_hi%d" % n) for n in range(2)]
        weigh_h(hi)
        for n, cols in enumerate((lo, hi)):
            nc.vector.tensor_tensor(numerator[n][:], y_sum[n][:], h_part[:, cols], ADD)
        for a, b in PIECES:
            nc.scalar.activation(inv_total[:, a:b], squared[:, a:b], ACT.Abs_reciprocal_sqrt, bias=1.0)
        for a, b in PIECES:
            nc.vector.scalar_tensor_tensor(
                result[:, a:b],
                inv_total[:, a:b],
                1.0 / RATIO_BOUND,
                numerator[a // HALF][:, a % HALF : a % HALF + b - a],
                MAX,
                MULT,
            )
            nc.sync.dma_start(out[:, a:b], result[:, a:b])
